import numpy as np
import ml_dtypes


def mxq(x, axis, fmt="e4m3"):
    dtype, down = {"e4m3": (ml_dtypes.float8_e4m3fn, 7), "e5m2": (ml_dtypes.float8_e5m2, 14)}[fmt]
    v = np.moveaxis(np.asarray(x, np.float32).astype(ml_dtypes.bfloat16).astype(np.float64), axis, -1)
    blocks = v.reshape(v.shape[:-1] + (-1, 32))
    amax = np.abs(blocks).max(-1, keepdims=True)
    byte = np.maximum(np.where(amax > 0, np.frexp(amax)[1] - 1 + 127, 0) - down, 1)
    scale = np.exp2(byte - 127.0)
    codes = (blocks / scale).astype(np.float32).astype(dtype).astype(np.float64)
    return np.moveaxis((codes * scale).reshape(v.shape), -1, axis)


WIDE = False


def mx_kscale(k):
    if not WIDE:
        return np.ones(k)
    levels = np.array([10, -10, 5, -5, 0])
    if k % 512:
        return np.exp2(np.random.permutation(np.resize(levels, k // 32))).repeat(32)
    a = np.empty((k // 512, 16))
    for p in range(k // 512):
        a[p, :8] = np.random.permutation(np.resize(levels, 8))
        for g in range(8):
            far = levels[np.abs(levels - a[p, g]) >= 10]
            a[p, g + 8] = far[np.random.randint(len(far))]
    return np.exp2(a.ravel()).repeat(32)


def f64(x):
    return np.asarray(x).astype(np.float64)


def striped(idx):
    return np.tile(np.asarray(idx).reshape(-1, 16).T, (8, 1)).astype(np.uint16)


def unstriped(offs):
    return offs[:16].T.reshape(-1).astype(np.int64)


E2M1 = np.array([0.0, 0.5, 1.0, 1.5, 2.0, 3.0, 4.0, 6.0, -0.0, -0.5, -1.0, -1.5, -2.0, -3.0, -4.0, -6.0])


def pack_weight(w, fmt):
    k, n = w.shape
    w = f64(np.asarray(w, np.float32).astype(ml_dtypes.bfloat16)).reshape(k // 32, 32, n)
    amax = np.abs(w).max(1)
    if fmt == "e4m3":
        byte = np.frexp(amax)[1] - 1 + 127 - 7
    else:
        mant, ex = np.frexp(amax / 6.0)
        byte = np.where(mant > 0.5, ex, ex - 1) + 127
    byte = np.clip(np.where(amax > 0, byte, 1), 1, 254)
    scaled = (w * np.exp2(127.0 - byte)[:, None, :]).reshape(k, n).astype(np.float32)
    by_word = np.ascontiguousarray(scaled.reshape(k // 512, 128, 4, n).transpose(0, 1, 3, 2))
    if fmt == "e4m3":
        words = by_word.astype(ml_dtypes.float8_e4m3fn).view(np.uint8)
    else:
        c = by_word.astype(ml_dtypes.float4_e2m1fn).view(np.uint8) & 0xF
        words = (c[..., 0::2] | (c[..., 1::2] << 4)).reshape(k // 512, 128, 2 * n)
    return np.ascontiguousarray(words), np.ascontiguousarray(byte.astype(np.uint8).reshape(k // 512, 16, n))


def unpack_weight(words, scales, fmt):
    g, _, n = scales.shape
    words = np.ascontiguousarray(words).reshape(g, 128, n, -1)
    if fmt == "e4m3":
        vals = words.view(ml_dtypes.float8_e4m3fn).astype(np.float64)
    else:
        nib = np.empty((g, 128, n, 4), np.uint8)
        nib[..., 0::2] = words & 0xF
        nib[..., 1::2] = words >> 4
        vals = E2M1[nib]
    vals = vals * np.repeat(np.exp2(scales.astype(np.float64) - 127.0), 8, axis=1)[..., None]
    return vals.transpose(0, 1, 3, 2).reshape(g * 512, n)


def bf(x):
    return np.asarray(x, np.float32).astype(ml_dtypes.bfloat16)


def planes(Y):
    r, m = Y.shape
    b = f64(bf(Y)).reshape(r // 32, 32, m)
    amax = np.abs(b).max(1)
    byte = np.clip(np.where(amax > 0, np.frexp(amax)[1] - 1 + 127 - 7, 1), 1, 254)
    codes = (b * np.exp2(127.0 - byte)[:, None, :]).reshape(r, m).astype(np.float32).astype(ml_dtypes.float8_e4m3fn).view(np.uint8)
    words = codes.reshape(r // 512, 128, 4, m).transpose(0, 1, 3, 2)
    return np.ascontiguousarray(words), np.ascontiguousarray(byte.astype(np.uint8).reshape(r // 512, 16, m))


D, T, I, J, U, Z, E = 512, 2048, 512, 512, 1024, 1024, 512


def setup_inputs():
    n = np.random.standard_normal
    idx = np.random.permutation(T)[:I]
    idx2 = np.random.permutation(U)[:J]
    idx3 = np.random.permutation(Z)[:J]
    fd = mx_kscale(D)
    fi = mx_kscale(I)
    ti = np.ones(T)
    ti[idx] = fi
    keysp = pack_weight(n((D, T)) / fd[:, None], "e2m1")
    return {
        "keys_words": keysp[0],
        "keys_scales": keysp[1],
        "notes": (n((D, U)) * 1.0 / np.sqrt(D) * fd[:, None]).astype(np.float32),
        "given": (np.random.uniform(0.3, 1.7, (I, Z))).astype(np.float32),
        "rowf": (np.random.uniform(0.02, 0.08, (I, 1)) * fi[:, None]).astype(np.float32),
        "vals": (n((E, T)) / ti).astype(np.float32),
        "mem": (np.random.uniform(0.3, 1.0, (1, J))).astype(np.float32),
        "offs": striped(idx),
        "offs2": striped(idx2),
        "offs3": striped(idx3),
    }


def reference(keys_words, keys_scales, notes, given, rowf, vals, mem, offs, offs2, offs3):
    idx = unstriped(offs)
    idx2 = unstriped(offs2)
    idx3 = unstriped(offs3)
    keysu = unpack_weight(keys_words, keys_scales, "e2m1")
    keysidxg = keysu[:, idx]
    notesidx2q = mxq(f64(notes)[:, idx2], 0, "e4m3")
    g1 = keysidxg.T @ notesidx2q
    g0 = g1 * f64(given)[:, idx3]
    gr1 = g0 * f64(rowf)
    vt1 = f64(vals)[:, idx].T
    vt1q = mxq(vt1, 0, "e4m3")
    gr1q = mxq(gr1, 0, "e4m3")
    o = vt1q.T @ gr1q
    o1 = np.pad(o, ((0, 0), (1, 0)))[:, :J]
    y = o - o1 * f64(mem)
    words, scales = planes(y)
    return y, words, scales

@@ -1,0 +1,205 @@
+from contextlib import ExitStack
+
+import concourse.mybir as mybir
+from concourse.masks import make_identity
+
+FLOPS = 2 * 2 * 512 * 512 * 512
+
+F32 = mybir.dt.float32
+BF16 = mybir.dt.bfloat16
+I32 = mybir.dt.int32
+U32 = mybir.dt.uint32
+U16 = mybir.dt.uint16
+U8 = mybir.dt.uint8
+FP8X4 = mybir.dt.float8_e4m3fn_x4
+FP4X4 = mybir.dt.float4_e2m1fn_x4
+MULT = mybir.AluOpType.mult
+SUBTRACT = mybir.AluOpType.subtract
+COPY = mybir.ActivationFunctionType.Copy
+
+P = 128
+PACK = 4
+N = 512
+TOKENS = 2048
+NOTES = 1024
+WIDE = 1024
+
+
+def interleave(engine, dst, src):
+    engine.tensor_copy(
+        out=dst.rearrange("p (c i) t -> p c t i", i=4),
+        in_=src.rearrange("p t (c i) -> p c t i", i=4),
+    )
+
+
+def tile_attend_tab_timestable_changes_pl_kernel(
+    tc, keys_words, keys_scales, notes, given, rowf, vals, mem, offs, offs2, offs3, out_0, out_1, out_2
+):
+    nc = tc.nc
+    with ExitStack() as ctx:
+        sb = ctx.enter_context(tc.tile_pool(name="sb", bufs=1))
+        acc = ctx.enter_context(tc.psum_pool(name="acc", bufs=4))
+        turn = ctx.enter_context(tc.psum_pool(name="turn", bufs=2))
+
+        idx = sb.tile([P, N // 16], U16, name="idx")
+        idx2 = sb.tile([P, N // 16], U16, name="idx2")
+        idx3 = sb.tile([P, N // 16], U16, name="idx3")
+        key_pool = sb.tile([P, TOKENS], U16, name="key_pool")
+        key_scale_pool = sb.tile([P, TOKENS], U8, name="key_scale_pool")
+        note_pool = [sb.tile([P, NOTES], F32, name="note_pool%d" % t) for t in range(PACK)]
+        given_pool = [sb.tile([P, WIDE], F32, name="given_pool%d" % t) for t in range(PACK)]
+        val_pool = [sb.tile([P, TOKENS], F32, name="val_pool%d" % t) for t in range(PACK)]
+        rowf_cols = sb.tile([P, PACK], F32, name="rowf_cols")
+        mem_cols = sb.tile([P, PACK], F32, name="mem_cols")
+
+        notes_by_place = notes.rearrange("(p t) u -> p t u", t=PACK)
+        given_by_place = given.rearrange("(p t) z -> p t z", t=PACK)
+        vals_by_place = vals.rearrange("(p t) c -> p t c", t=PACK)
+        out_by_place = out_0.rearrange("(p t) j -> p t j", t=PACK)
+
+        nc.vector.memset(key_scale_pool[:].bitcast(I32), 0)
+        identity = sb.tile([P, P], F32, name="identity")
+        make_identity(nc, identity[:])
+
+        def load_key_scales(q):
+            nc.sync.dma_start(
+                out=key_scale_pool[32 * q : 32 * q + 4, :].bitcast(I32),
+                in_=keys_scales[0, 4 * q : 4 * q + 4, :].bitcast(I32),
+            )
+
+        nc.sync.dma_start(idx2[:], offs2)
+        nc.sync.dma_start(out=note_pool[0][:], in_=notes_by_place[:, 0, :])
+        nc.sync.dma_start(out=note_pool[1][:], in_=notes_by_place[:, 1, :])
+        nc.sync.dma_start(out=key_pool[:].bitcast(I32), in_=keys_words[0].bitcast(I32))
+        nc.sync.dma_start(out=note_pool[2][:], in_=notes_by_place[:, 2, :])
+        nc.sync.dma_start(idx[:], offs)
+        for q in range(4):
+            load_key_scales(q)
+        nc.sync.dma_start(out=note_pool[3][:], in_=notes_by_place[:, 3, :])
+        nc.sync.dma_start(out=given_pool[0][:], in_=given_by_place[:, 0, :])
+        nc.sync.dma_start(idx3[:], offs3)
+        nc.sync.dma_start(out=given_pool[1][:], in_=given_by_place[:, 1, :])
+        nc.sync.dma_start(out=rowf_cols[:], in_=rowf.rearrange("(p t) o -> p (t o)", t=PACK))
+        nc.sync.dma_start(out=given_pool[2][:], in_=given_by_place[:, 2, :])
+        nc.sync.dma_start(out=mem_cols[:], in_=mem.rearrange("o (p t) -> p (o t)", t=PACK))
+        nc.sync.dma_start(out=given_pool[3][:], in_=given_by_place[:, 3, :])
+        for t in range(PACK):
+            nc.sync.dma_start(out=val_pool[t][:], in_=vals_by_place[:, t, :])
+
+        shifted = sb.tile([P, N], F32, name="shifted")
+        nc.vector.memset(shifted[:, 0:1], 0.0)
+
+        note_planes = sb.tile([P, PACK, N], BF16, name="note_planes")
+        for t in range(PACK):
+            nc.scalar.activation(note_planes[:, t, :], note_pool[t][:].indirect(idx2[:]), COPY)
+
+        key_listed = sb.tile([P, N], U16, name="key_listed")
+        nc.vector.tensor_copy(key_listed[:], key_pool[:].indirect(idx[:]))
+        key_scales = sb.tile([P, PACK, P], U8, name="key_scales", align_bytes=64)
+        nc.vector.tensor_copy(key_scales[:].rearrange("p r s -> p s r"), key_scale_pool[:].indirect(idx[:]))
+        key_words = sb.tile([P, 2 * N], U8, name="key_words", align_bytes=64)
+        nc.vector.tensor_copy(
+            out=key_words[:].bitcast(U16).rearrange("p (r s) -> p r s", r=PACK),
+            in_=key_listed[:].rearrange("p (s r) -> p r s", r=PACK),
+        )
+
+        note_grouped = sb.tile([P, N, PACK], BF16, name="note_grouped", align_bytes=64)
+        interleave(nc.vector, note_grouped[:], note_planes[:])
+        note_codes = sb.tile([P, N], U32, name="note_codes", align_bytes=64)
+        note_scales = sb.tile([P, N], U8, name="note_scales", align_bytes=64)
+        nc.vector.quantize_mx(
+            out=note_codes[:].bitcast(FP8X4),
+            scales=note_scales[:],
+            in_=note_grouped[:].rearrange("p j t -> p (j t)"),
+        )
+
+        given_listed = sb.tile([P, PACK, N], F32, name="given_listed")
+        for r in range(PACK):
+            nc.scalar.activation(given_listed[:, r, :], given_pool[r][:].indirect(idx3[:]), COPY)
+
+        mem_turned = turn.tile([P, PACK, P], F32, name="mem_turned", tag="turn")
+        for c in range(PACK):
+            nc.tensor.transpose(mem_turned[:, c, :], mem_cols[:, c : c + 1].to_broadcast([P, P]), identity[:])
+        mem_row = sb.tile([P, N], F32, name="mem_row")
+        nc.vector.tensor_copy(
+            out=mem_row[:].rearrange("p (n c) -> p n c", c=PACK), in_=mem_turned[:].rearrange("p c n -> p n c")
+        )
+
+        table_planes = sb.tile([P, PACK, N], BF16, name="table_planes")
+        for r in range(PACK):
+            g1 = acc.tile([P, N], F32, name="g1", tag="acc")
+            nc.tensor.matmul_mx(
+                out=g1[:],
+                lhsT=key_words[:, 2 * P * r : 2 * P * (r + 1)].bitcast(FP4X4),
+                lhsT_scale=key_scales[:, r, :],
+                rhs=note_codes[:].bitcast(FP8X4),
+                rhs_scale=note_scales[:],
+                start=True,
+                stop=True,
+            )
+            nc.vector.scalar_tensor_tensor(
+                out=table_planes[:, r, :],
+                in0=g1[:],
+                scalar=rowf_cols[:, r : r + 1],
+                in1=given_listed[:, r, :],
+                op0=MULT,
+                op1=MULT,
+            )
+        table_grouped = sb.tile([P, N, PACK], BF16, name="table_grouped", align_bytes=64)
+        interleave(nc.vector, table_grouped[:], table_planes[:])
+        table_codes = sb.tile([P, N], U32, name="table_codes", align_bytes=64)
+        table_scales = sb.tile([P, N], U8, name="table_scales", align_bytes=64)
+        nc.vector.quantize_mx(
+            out=table_codes[:].bitcast(FP8X4),
+            scales=table_scales[:],
+            in_=table_grouped[:].rearrange("p j t -> p (j t)"),
+        )
+
+        result = sb.tile([P, PACK, N], F32, name="result")
+        for t in range(PACK):
+            val_listed = sb.tile([P, N], BF16, name="val_listed%d" % t)
+            nc.scalar.activation(val_listed[:], val_pool[t][:].indirect(idx[:]), COPY)
+            pairs = val_listed[:].bitcast(F32)
+            val_turned = turn.tile([P, PACK, P], F32, name="val_turned", tag="turn")
+            for u in range(2):
+                nc.tensor.transpose(val_turned[:, u, :], pairs[:, u : N // 2 : 2], identity[:])
+            val_grouped = sb.tile([P, P * PACK], BF16, name="val_grouped%d" % t, align_bytes=64)
+            nc.scalar.copy(
+                out=val_grouped[:].bitcast(F32).rearrange("s (p u) -> s p u", u=2),
+                in_=val_turned[:, 0:2, :].rearrange("s u p -> s p u"),
+            )
+            val_codes = sb.tile([P, P], U32, name="val_codes%d" % t, align_bytes=64)
+            val_scales = sb.tile([P, P], U8, name="val_scales%d" % t, align_bytes=64)
+            nc.vector.quantize_mx(out=val_codes[:].bitcast(FP8X4), scales=val_scales[:], in_=val_grouped[:])
+            o = acc.tile([P, N], F32, name="o", tag="acc")
+            nc.tensor.matmul_mx(
+                out=o[:],
+                lhsT=val_codes[:].bitcast(FP8X4),
+                lhsT_scale=val_scales[:],
+                rhs=table_codes[:].bitcast(FP8X4),
+                rhs_scale=table_scales[:],
+                start=True,
+                stop=True,
+            )
+            nc.vector.tensor_tensor(shifted[:, 1:N], o[:, 0 : N - 1], mem_row[:, 1:N], MULT)
+            nc.vector.tensor_tensor(result[:, t, :], o[:], shifted[:], SUBTRACT)
+            nc.sync.dma_start(out=out_by_place[:, t, :], in_=result[:, t, :])
+
+        result_grouped = sb.tile([P, N, PACK], BF16, name="result_grouped", align_bytes=64)
+        interleave(nc.vector, result_grouped[:], result[:])
+        result_codes = sb.tile([P, N], U32, name="result_codes", align_bytes=64)
+        result_scales = sb.tile([P, N], U8, name="result_scales", align_bytes=64)
+        nc.vector.quantize_mx(
+            out=result_codes[:].bitcast(FP8X4),
+            scales=result_scales[:],
+            in_=result_grouped[:].rearrange("p j t -> p (j t)"),
+        )
+        nc.sync.dma_start(
+            out=out_1[0].rearrange("p c r -> p (c r)").bitcast(I32), in_=result_codes[:].bitcast(I32)
+        )
+        for q in range(4):
+            queue = nc.scalar if q % 2 else nc.sync
+            queue.dma_start(
+                out=out_2[0, 4 * q : 4 * q + 4, :].bitcast(I32),
+                in_=result_scales[32 * q : 32 * q + 4, :].bitcast(I32),
+            )

@@ -25,10 +25,23 @@ NOTES = 1024
 WIDE = 1024
 
 
-def interleave(engine, dst, src):
-    engine.tensor_copy(
-        out=dst.rearrange("p (c i) t -> p c t i", i=4),
-        in_=src.rearrange("p t (c i) -> p c t i", i=4),
+HALF = N // 2
+HALVES = [slice(0, HALF), slice(HALF, N)]
+
+
+def interleave(nc, grouped, planes):
+    for cols in HALVES:
+        nc.vector.tensor_copy(
+            out=grouped[:, cols, :].rearrange("p (c i) t -> p c t i", i=4),
+            in_=planes[:, :, cols].rearrange("p t (c i) -> p c t i", i=4),
+        )
+
+
+def quantise(nc, codes, scales, grouped, cols):
+    nc.vector.quantize_mx(
+        out=codes[:, cols].bitcast(FP8X4),
+        scales=scales[:, cols],
+        in_=grouped[:, cols, :].rearrange("p j t -> p (j t)"),
     )
 
 
@@ -38,7 +51,7 @@ def tile_attend_tab_timestable_changes_pl_kernel(
     nc = tc.nc
     with ExitStack() as ctx:
         sb = ctx.enter_context(tc.tile_pool(name="sb", bufs=1))
-        acc = ctx.enter_context(tc.psum_pool(name="acc", bufs=4))
+        acc = ctx.enter_context(tc.psum_pool(name="acc", bufs=6))
         turn = ctx.enter_context(tc.psum_pool(name="turn", bufs=2))
 
         idx = sb.tile([P, N // 16], U16, name="idx")
@@ -57,6 +70,8 @@ def tile_attend_tab_timestable_changes_pl_kernel(
         vals_by_place = vals.rearrange("(p t) c -> p t c", t=PACK)
         out_by_place = out_0.rearrange("(p t) j -> p t j", t=PACK)
 
+        zero = sb.tile([P, 1], F32, name="zero")
+        nc.vector.memset(zero[:], 0.0)
         nc.vector.memset(key_scale_pool[:].bitcast(I32), 0)
         identity = sb.tile([P, P], F32, name="identity")
         make_identity(nc, identity[:])
@@ -67,13 +82,15 @@ def tile_attend_tab_timestable_changes_pl_kernel(
                 in_=keys_scales[0, 4 * q : 4 * q + 4, :].bitcast(I32),
             )
 
+        nc.sync.dma_start(out=mem_cols[:], in_=mem.rearrange("o (p t) -> p (o t)", t=PACK))
         nc.sync.dma_start(idx2[:], offs2)
         nc.sync.dma_start(out=note_pool[0][:], in_=notes_by_place[:, 0, :])
         nc.sync.dma_start(out=note_pool[1][:], in_=notes_by_place[:, 1, :])
-        nc.sync.dma_start(out=key_pool[:].bitcast(I32), in_=keys_words[0].bitcast(I32))
-        nc.sync.dma_start(out=note_pool[2][:], in_=notes_by_place[:, 2, :])
         nc.sync.dma_start(idx[:], offs)
-        for q in range(4):
+        nc.sync.dma_start(out=key_pool[:].bitcast(I32), in_=keys_words[0].bitcast(I32))
+        load_key_scales(0)
+        nc.sync.dma_start(out=note_pool[2][:], in_=notes_by_place[:, 2, :])
+        for q in range(1, 4):
             load_key_scales(q)
         nc.sync.dma_start(out=note_pool[3][:], in_=notes_by_place[:, 3, :])
         nc.sync.dma_start(out=given_pool[0][:], in_=given_by_place[:, 0, :])
@@ -81,13 +98,12 @@ def tile_attend_tab_timestable_changes_pl_kernel(
         nc.sync.dma_start(out=given_pool[1][:], in_=given_by_place[:, 1, :])
         nc.sync.dma_start(out=rowf_cols[:], in_=rowf.rearrange("(p t) o -> p (t o)", t=PACK))
         nc.sync.dma_start(out=given_pool[2][:], in_=given_by_place[:, 2, :])
-        nc.sync.dma_start(out=mem_cols[:], in_=mem.rearrange("o (p t) -> p (o t)", t=PACK))
         nc.sync.dma_start(out=given_pool[3][:], in_=given_by_place[:, 3, :])
         for t in range(PACK):
             nc.sync.dma_start(out=val_pool[t][:], in_=vals_by_place[:, t, :])
 
         shifted = sb.tile([P, N], F32, name="shifted")
-        nc.vector.memset(shifted[:, 0:1], 0.0)
+        nc.scalar.activation(shifted[:, 0:1], zero[:], COPY)
 
         note_planes = sb.tile([P, PACK, N], BF16, name="note_planes")
         for t in range(PACK):
@@ -104,14 +120,11 @@ def tile_attend_tab_timestable_changes_pl_kernel(
         )
 
         note_grouped = sb.tile([P, N, PACK], BF16, name="note_grouped", align_bytes=64)
-        interleave(nc.vector, note_grouped[:], note_planes[:])
+        interleave(nc, note_grouped, note_planes)
         note_codes = sb.tile([P, N], U32, name="note_codes", align_bytes=64)
         note_scales = sb.tile([P, N], U8, name="note_scales", align_bytes=64)
-        nc.vector.quantize_mx(
-            out=note_codes[:].bitcast(FP8X4),
-            scales=note_scales[:],
-            in_=note_grouped[:].rearrange("p j t -> p (j t)"),
-        )
+        for cols in HALVES:
+            quantise(nc, note_codes, note_scales, note_grouped, cols)
 
         given_listed = sb.tile([P, PACK, N], F32, name="given_listed")
         for r in range(PACK):
@@ -146,59 +159,66 @@ def tile_attend_tab_timestable_changes_pl_kernel(
                 op1=MULT,
             )
         table_grouped = sb.tile([P, N, PACK], BF16, name="table_grouped", align_bytes=64)
-        interleave(nc.vector, table_grouped[:], table_planes[:])
+        interleave(nc, table_grouped, table_planes)
         table_codes = sb.tile([P, N], U32, name="table_codes", align_bytes=64)
         table_scales = sb.tile([P, N], U8, name="table_scales", align_bytes=64)
-        nc.vector.quantize_mx(
-            out=table_codes[:].bitcast(FP8X4),
-            scales=table_scales[:],
-            in_=table_grouped[:].rearrange("p j t -> p (j t)"),
-        )
+        for cols in HALVES:
+            quantise(nc, table_codes, table_scales, table_grouped, cols)
 
         result = sb.tile([P, PACK, N], F32, name="result")
+        result_codes = sb.tile([P, N], U32, name="result_codes", align_bytes=64)
+        result_scales = sb.tile([P, N], U8, name="result_scales", align_bytes=64)
         for t in range(PACK):
-            val_listed = sb.tile([P, N], BF16, name="val_listed%d" % t)
+            val_listed = sb.tile([P, N], BF16, name="val_listed%d" % t, tag="val_listed%d" % t, align_bytes=64)
             nc.scalar.activation(val_listed[:], val_pool[t][:].indirect(idx[:]), COPY)
             pairs = val_listed[:].bitcast(F32)
             val_turned = turn.tile([P, PACK, P], F32, name="val_turned", tag="turn")
             for u in range(2):
                 nc.tensor.transpose(val_turned[:, u, :], pairs[:, u : N // 2 : 2], identity[:])
             val_grouped = sb.tile([P, P * PACK], BF16, name="val_grouped%d" % t, align_bytes=64)
-            nc.scalar.copy(
+            copy_words = nc.scalar.copy if t % 2 else nc.vector.tensor_copy
+            copy_words(
                 out=val_grouped[:].bitcast(F32).rearrange("s (p u) -> s p u", u=2),
                 in_=val_turned[:, 0:2, :].rearrange("s u p -> s p u"),
             )
             val_codes = sb.tile([P, P], U32, name="val_codes%d" % t, align_bytes=64)
             val_scales = sb.tile([P, P], U8, name="val_scales%d" % t, align_bytes=64)
             nc.vector.quantize_mx(out=val_codes[:].bitcast(FP8X4), scales=val_scales[:], in_=val_grouped[:])
-            o = acc.tile([P, N], F32, name="o", tag="acc")
-            nc.tensor.matmul_mx(
-                out=o[:],
-                lhsT=val_codes[:].bitcast(FP8X4),
-                lhsT_scale=val_scales[:],
-                rhs=table_codes[:].bitcast(FP8X4),
-                rhs_scale=table_scales[:],
-                start=True,
-                stop=True,
-            )
-            nc.vector.tensor_tensor(shifted[:, 1:N], o[:, 0 : N - 1], mem_row[:, 1:N], MULT)
-            nc.vector.tensor_tensor(result[:, t, :], o[:], shifted[:], SUBTRACT)
+            sums = []
+            for cols in HALVES:
+                o = acc.tile([P, N], F32, name="o", tag="acc")
+                nc.tensor.matmul_mx(
+                    out=o[:, 0:HALF],
+                    lhsT=val_codes[:].bitcast(FP8X4),
+                    lhsT_scale=val_scales[:],
+                    rhs=table_codes[:, cols].bitcast(FP8X4),
+                    rhs_scale=table_scales[:, cols],
+                    start=True,
+                    stop=True,
+                )
+                sums.append(o)
+            for cols, o in zip(HALVES, sums):
+                after = slice(cols.start + 1, min(cols.stop + 1, N))
+                nc.vector.tensor_tensor(
+                    shifted[:, after], o[:, 0 : after.stop - after.start], mem_row[:, after], MULT
+                )
+            for cols, o in zip(HALVES, sums):
+                nc.vector.tensor_tensor(result[:, t, cols], o[:, 0:HALF], shifted[:, cols], SUBTRACT)
             nc.sync.dma_start(out=out_by_place[:, t, :], in_=result[:, t, :])
 
-        result_grouped = sb.tile([P, N, PACK], BF16, name="result_grouped", align_bytes=64)
-        interleave(nc.vector, result_grouped[:], result[:])
-        result_codes = sb.tile([P, N], U32, name="result_codes", align_bytes=64)
-        result_scales = sb.tile([P, N], U8, name="result_scales", align_bytes=64)
-        nc.vector.quantize_mx(
-            out=result_codes[:].bitcast(FP8X4),
-            scales=result_scales[:],
-            in_=result_grouped[:].rearrange("p j t -> p (j t)"),
+        result_grouped = sb.tile(
+            [P, N, PACK], BF16, name="result_grouped", tag="val_listed%d" % (PACK - 1), align_bytes=64
         )
-        nc.sync.dma_start(
-            out=out_1[0].rearrange("p c r -> p (c r)").bitcast(I32), in_=result_codes[:].bitcast(I32)
-        )
+        for pair, copy in ((slice(0, 2), nc.scalar.copy), (slice(2, 4), nc.vector.tensor_copy)):
+            for cols in HALVES:
+                copy(out=result_grouped[:, cols, pair], in_=result[:, pair, cols].rearrange("p t j -> p j t"))
+
+        words_out = out_1[0].rearrange("p c r -> p (c r)").bitcast(I32)
+        for cols in HALVES:
+            quantise(nc, result_codes, result_scales, result_grouped, cols)
+            nc.sync.dma_start(out=words_out[:, cols], in_=result_codes[:, cols].bitcast(I32))
         for q in range(4):
-            queue = nc.scalar if q % 2 else nc.sync
+            queue = nc.scalar if q else nc.sync
             queue.dma_start(
                 out=out_2[0, 4 * q : 4 * q + 4, :].bitcast(I32),
                 in_=result_scales[32 * q : 32 * q + 4, :].bitcast(I32),

@@ -37,6 +37,11 @@ def interleave(nc, grouped, planes):
         )
 
 
+def interleave_pair(copy, grouped, planes, pair):
+    for cols in HALVES:
+        copy(out=grouped[:, cols, pair], in_=planes[:, pair, cols].rearrange("p t j -> p j t"))
+
+
 def quantise(nc, codes, scales, grouped, cols):
     nc.vector.quantize_mx(
         out=codes[:, cols].bitcast(FP8X4),
@@ -59,9 +64,9 @@ def tile_attend_tab_timestable_changes_pl_kernel(
         idx3 = sb.tile([P, N // 16], U16, name="idx3")
         key_pool = sb.tile([P, TOKENS], U16, name="key_pool")
         key_scale_pool = sb.tile([P, TOKENS], U8, name="key_scale_pool")
-        note_pool = [sb.tile([P, NOTES], F32, name="note_pool%d" % t) for t in range(PACK)]
+        note_pool = [sb.tile([P, 2, NOTES], F32, name="note_pool%d" % u) for u in range(2)]
         given_pool = [sb.tile([P, WIDE], F32, name="given_pool%d" % t) for t in range(PACK)]
-        val_pool = [sb.tile([P, TOKENS], F32, name="val_pool%d" % t) for t in range(PACK)]
+        val_pool = [sb.tile([P, TOKENS], F32, name="val_pool%d" % t, tag="val_pool%d" % t, align_bytes=64) for t in range(PACK)]
         rowf_cols = sb.tile([P, PACK], F32, name="rowf_cols")
         mem_cols = sb.tile([P, PACK], F32, name="mem_cols")
 
@@ -82,17 +87,14 @@ def tile_attend_tab_timestable_changes_pl_kernel(
                 in_=keys_scales[0, 4 * q : 4 * q + 4, :].bitcast(I32),
             )
 
-        nc.sync.dma_start(out=mem_cols[:], in_=mem.rearrange("o (p t) -> p (o t)", t=PACK))
-        nc.sync.dma_start(idx2[:], offs2)
-        nc.sync.dma_start(out=note_pool[0][:], in_=notes_by_place[:, 0, :])
-        nc.sync.dma_start(out=note_pool[1][:], in_=notes_by_place[:, 1, :])
         nc.sync.dma_start(idx[:], offs)
         nc.sync.dma_start(out=key_pool[:].bitcast(I32), in_=keys_words[0].bitcast(I32))
-        load_key_scales(0)
-        nc.sync.dma_start(out=note_pool[2][:], in_=notes_by_place[:, 2, :])
-        for q in range(1, 4):
+        for q in range(4):
             load_key_scales(q)
-        nc.sync.dma_start(out=note_pool[3][:], in_=notes_by_place[:, 3, :])
+        nc.sync.dma_start(out=note_pool[0][:], in_=notes_by_place[:, 0:2, :])
+        nc.sync.dma_start(idx2[:], offs2)
+        nc.sync.dma_start(out=note_pool[1][:], in_=notes_by_place[:, 2:4, :])
+        nc.sync.dma_start(out=mem_cols[:], in_=mem.rearrange("o (p t) -> p (o t)", t=PACK))
         nc.sync.dma_start(out=given_pool[0][:], in_=given_by_place[:, 0, :])
         nc.sync.dma_start(idx3[:], offs3)
         nc.sync.dma_start(out=given_pool[1][:], in_=given_by_place[:, 1, :])
@@ -105,10 +107,6 @@ def tile_attend_tab_timestable_changes_pl_kernel(
         shifted = sb.tile([P, N], F32, name="shifted")
         nc.scalar.activation(shifted[:, 0:1], zero[:], COPY)
 
-        note_planes = sb.tile([P, PACK, N], BF16, name="note_planes")
-        for t in range(PACK):
-            nc.scalar.activation(note_planes[:, t, :], note_pool[t][:].indirect(idx2[:]), COPY)
-
         key_listed = sb.tile([P, N], U16, name="key_listed")
         nc.vector.tensor_copy(key_listed[:], key_pool[:].indirect(idx[:]))
         key_scales = sb.tile([P, PACK, P], U8, name="key_scales", align_bytes=64)
@@ -119,16 +117,16 @@ def tile_attend_tab_timestable_changes_pl_kernel(
             in_=key_listed[:].rearrange("p (s r) -> p r s", r=PACK),
         )
 
+        note_planes = sb.tile([P, PACK, N], F32, name="note_planes")
         note_grouped = sb.tile([P, N, PACK], BF16, name="note_grouped", align_bytes=64)
-        interleave(nc, note_grouped, note_planes)
+        for u in range(2):
+            nc.scalar.activation(note_planes[:, 2 * u, :], note_pool[u][:, 0, :].indirect(idx2[:]), COPY)
+            nc.vector.tensor_copy(note_planes[:, 2 * u + 1, :], note_pool[u][:, 1, :].indirect(idx2[:]))
+            interleave_pair(nc.vector.tensor_copy, note_grouped, note_planes, slice(2 * u, 2 * u + 2))
         note_codes = sb.tile([P, N], U32, name="note_codes", align_bytes=64)
         note_scales = sb.tile([P, N], U8, name="note_scales", align_bytes=64)
         for cols in HALVES:
             quantise(nc, note_codes, note_scales, note_grouped, cols)
-
-        given_listed = sb.tile([P, PACK, N], F32, name="given_listed")
-        for r in range(PACK):
-            nc.scalar.activation(given_listed[:, r, :], given_pool[r][:].indirect(idx3[:]), COPY)
 
         mem_turned = turn.tile([P, PACK, P], F32, name="mem_turned", tag="turn")
         for c in range(PACK):
@@ -138,6 +136,11 @@ def tile_attend_tab_timestable_changes_pl_kernel(
             out=mem_row[:].rearrange("p (n c) -> p n c", c=PACK), in_=mem_turned[:].rearrange("p c n -> p n c")
         )
 
+        given_listed = sb.tile([P, PACK, N], F32, name="given_listed")
+        for r in range(PACK):
+            nc.scalar.activation(given_listed[:, r, :], given_pool[r][:].indirect(idx3[:]), COPY)
+
+        table_grouped = sb.tile([P, N, PACK], BF16, name="table_grouped", align_bytes=64)
         table_planes = sb.tile([P, PACK, N], BF16, name="table_planes")
         for r in range(PACK):
             g1 = acc.tile([P, N], F32, name="g1", tag="acc")
@@ -158,7 +161,6 @@ def tile_attend_tab_timestable_changes_pl_kernel(
                 op0=MULT,
                 op1=MULT,
             )
-        table_grouped = sb.tile([P, N, PACK], BF16, name="table_grouped", align_bytes=64)
         interleave(nc, table_grouped, table_planes)
         table_codes = sb.tile([P, N], U32, name="table_codes", align_bytes=64)
         table_scales = sb.tile([P, N], U8, name="table_scales", align_bytes=64)
@@ -168,29 +170,38 @@ def tile_attend_tab_timestable_changes_pl_kernel(
         result = sb.tile([P, PACK, N], F32, name="result")
         result_codes = sb.tile([P, N], U32, name="result_codes", align_bytes=64)
         result_scales = sb.tile([P, N], U8, name="result_scales", align_bytes=64)
-        for t in range(PACK):
-            val_listed = sb.tile([P, N], BF16, name="val_listed%d" % t, tag="val_listed%d" % t, align_bytes=64)
-            nc.scalar.activation(val_listed[:], val_pool[t][:].indirect(idx[:]), COPY)
-            pairs = val_listed[:].bitcast(F32)
-            val_turned = turn.tile([P, PACK, P], F32, name="val_turned", tag="turn")
+        last = PACK - 1
+        val_codes, val_scales = {}, {}
+
+        def prepare_values(t):
+            listed = sb.tile([P, N], BF16, name="val_listed%d" % t, tag="val_listed%d" % t, align_bytes=64)
+            nc.scalar.activation(listed[:], val_pool[t][:].indirect(idx[:]), COPY)
+            pairs = listed[:].bitcast(F32)
+            turned = turn.tile([P, PACK, P], F32, name="val_turned", tag="turn")
             for u in range(2):
-                nc.tensor.transpose(val_turned[:, u, :], pairs[:, u : N // 2 : 2], identity[:])
-            val_grouped = sb.tile([P, P * PACK], BF16, name="val_grouped%d" % t, align_bytes=64)
+                nc.tensor.transpose(turned[:, u, :], pairs[:, u : N // 2 : 2], identity[:])
+            grouped = sb.tile([P, P * PACK], BF16, name="val_grouped%d" % t, align_bytes=64)
             copy_words = nc.scalar.copy if t % 2 else nc.vector.tensor_copy
             copy_words(
-                out=val_grouped[:].bitcast(F32).rearrange("s (p u) -> s p u", u=2),
-                in_=val_turned[:, 0:2, :].rearrange("s u p -> s p u"),
+                out=grouped[:].bitcast(F32).rearrange("s (p u) -> s p u", u=2),
+                in_=turned[:, 0:2, :].rearrange("s u p -> s p u"),
             )
-            val_codes = sb.tile([P, P], U32, name="val_codes%d" % t, align_bytes=64)
-            val_scales = sb.tile([P, P], U8, name="val_scales%d" % t, align_bytes=64)
-            nc.vector.quantize_mx(out=val_codes[:].bitcast(FP8X4), scales=val_scales[:], in_=val_grouped[:])
+            return grouped
+
+        def quantise_values(t, grouped):
+            tag = "val_pool%d" % last if t == last - 1 else "val_codes%d" % t
+            val_codes[t] = sb.tile([P, P], U32, name="val_codes%d" % t, tag=tag, align_bytes=64)
+            val_scales[t] = sb.tile([P, P], U8, name="val_scales%d" % t, align_bytes=64)
+            nc.vector.quantize_mx(out=val_codes[t][:].bitcast(FP8X4), scales=val_scales[t][:], in_=grouped[:])
+
+        def finish_rows(t):
             sums = []
             for cols in HALVES:
                 o = acc.tile([P, N], F32, name="o", tag="acc")
                 nc.tensor.matmul_mx(
                     out=o[:, 0:HALF],
-                    lhsT=val_codes[:].bitcast(FP8X4),
-                    lhsT_scale=val_scales[:],
+                    lhsT=val_codes[t][:].bitcast(FP8X4),
+                    lhsT_scale=val_scales[t][:],
                     rhs=table_codes[:, cols].bitcast(FP8X4),
                     rhs_scale=table_scales[:, cols],
                     start=True,
@@ -206,12 +217,17 @@ def tile_attend_tab_timestable_changes_pl_kernel(
                 nc.vector.tensor_tensor(result[:, t, cols], o[:, 0:HALF], shifted[:, cols], SUBTRACT)
             nc.sync.dma_start(out=out_by_place[:, t, :], in_=result[:, t, :])
 
+        grouped = [prepare_values(t) for t in range(PACK)]
+        for t in range(PACK):
+            quantise_values(t, grouped[t])
+        for t in range(PACK):
+            finish_rows(t)
+
         result_grouped = sb.tile(
             [P, N, PACK], BF16, name="result_grouped", tag="val_listed%d" % (PACK - 1), align_bytes=64
         )
-        for pair, copy in ((slice(0, 2), nc.scalar.copy), (slice(2, 4), nc.vector.tensor_copy)):
-            for cols in HALVES:
-                copy(out=result_grouped[:, cols, pair], in_=result[:, pair, cols].rearrange("p t j -> p j t"))
+        interleave_pair(nc.scalar.copy, result_grouped, result, slice(0, 2))
+        interleave_pair(nc.vector.tensor_copy, result_grouped, result, slice(2, 4))
 
         words_out = out_1[0].rearrange("p c r -> p (c r)").bitcast(I32)
         for cols in HALVES:

@@ -18,18 +18,22 @@ SUBTRACT = mybir.AluOpType.subtract
 COPY = mybir.ActivationFunctionType.Copy
 
 P = 128
-PACK = 4
+PLACES = 4
+LAST = PLACES - 1
+QUADRANTS = 4
 N = 512
 TOKENS = 2048
 NOTES = 1024
 WIDE = 1024
 
-
 HALF = N // 2
 HALVES = [slice(0, HALF), slice(HALF, N)]
+SCALAR_SHARE = N // 4
+SUM_BANKS = 6
+TURN_BANKS = 2
 
 
-def interleave(nc, grouped, planes):
+def group_planes(nc, grouped, planes):
     for cols in HALVES:
         nc.vector.tensor_copy(
             out=grouped[:, cols, :].rearrange("p (c i) t -> p c t i", i=4),
@@ -37,9 +41,8 @@ def interleave(nc, grouped, planes):
         )
 
 
-def interleave_pair(copy, grouped, planes, pair):
-    for cols in HALVES:
-        copy(out=grouped[:, cols, pair], in_=planes[:, pair, cols].rearrange("p t j -> p j t"))
+def group_pair(copy, grouped, planes, pair, cols):
+    copy(out=grouped[:, cols, pair], in_=planes[:, pair, cols].rearrange("p t j -> p j t"))
 
 
 def quantise(nc, codes, scales, grouped, cols):
@@ -56,8 +59,8 @@ def tile_attend_tab_timestable_changes_pl_kernel(
     nc = tc.nc
     with ExitStack() as ctx:
         sb = ctx.enter_context(tc.tile_pool(name="sb", bufs=1))
-        acc = ctx.enter_context(tc.psum_pool(name="acc", bufs=6))
-        turn = ctx.enter_context(tc.psum_pool(name="turn", bufs=2))
+        acc = ctx.enter_context(tc.psum_pool(name="acc", bufs=SUM_BANKS))
+        turn = ctx.enter_context(tc.psum_pool(name="turn", bufs=TURN_BANKS))
 
         idx = sb.tile([P, N // 16], U16, name="idx")
         idx2 = sb.tile([P, N // 16], U16, name="idx2")
@@ -65,15 +68,18 @@ def tile_attend_tab_timestable_changes_pl_kernel(
         key_pool = sb.tile([P, TOKENS], U16, name="key_pool")
         key_scale_pool = sb.tile([P, TOKENS], U8, name="key_scale_pool")
         note_pool = [sb.tile([P, 2, NOTES], F32, name="note_pool%d" % u) for u in range(2)]
-        given_pool = [sb.tile([P, WIDE], F32, name="given_pool%d" % t) for t in range(PACK)]
-        val_pool = [sb.tile([P, TOKENS], F32, name="val_pool%d" % t, tag="val_pool%d" % t, align_bytes=64) for t in range(PACK)]
-        rowf_cols = sb.tile([P, PACK], F32, name="rowf_cols")
-        mem_cols = sb.tile([P, PACK], F32, name="mem_cols")
+        given_pool = [sb.tile([P, WIDE], F32, name="given_pool%d" % t) for t in range(PLACES)]
+        val_pool = [
+            sb.tile([P, TOKENS], F32, name="val_pool%d" % t, tag="val_pool%d" % t, align_bytes=64)
+            for t in range(PLACES)
+        ]
+        rowf_cols = sb.tile([P, PLACES], F32, name="rowf_cols")
+        mem_cols = sb.tile([P, PLACES], F32, name="mem_cols")
 
-        notes_by_place = notes.rearrange("(p t) u -> p t u", t=PACK)
-        given_by_place = given.rearrange("(p t) z -> p t z", t=PACK)
-        vals_by_place = vals.rearrange("(p t) c -> p t c", t=PACK)
-        out_by_place = out_0.rearrange("(p t) j -> p t j", t=PACK)
+        notes_by_place = notes.rearrange("(p t) u -> p t u", t=PLACES)
+        given_by_place = given.rearrange("(p t) z -> p t z", t=PLACES)
+        vals_by_place = vals.rearrange("(p t) c -> p t c", t=PLACES)
+        out_by_place = out_0.rearrange("(p t) j -> p t j", t=PLACES)
 
         zero = sb.tile([P, 1], F32, name="zero")
         nc.vector.memset(zero[:], 0.0)
@@ -81,27 +87,24 @@ def tile_attend_tab_timestable_changes_pl_kernel(
         identity = sb.tile([P, P], F32, name="identity")
         make_identity(nc, identity[:])
 
-        def load_key_scales(q):
+        nc.sync.dma_start(idx[:], offs)
+        nc.sync.dma_start(out=key_pool[:].bitcast(I32), in_=keys_words[0].bitcast(I32))
+        for q in range(QUADRANTS):
             nc.sync.dma_start(
                 out=key_scale_pool[32 * q : 32 * q + 4, :].bitcast(I32),
                 in_=keys_scales[0, 4 * q : 4 * q + 4, :].bitcast(I32),
             )
-
-        nc.sync.dma_start(idx[:], offs)
-        nc.sync.dma_start(out=key_pool[:].bitcast(I32), in_=keys_words[0].bitcast(I32))
-        for q in range(4):
-            load_key_scales(q)
         nc.sync.dma_start(out=note_pool[0][:], in_=notes_by_place[:, 0:2, :])
         nc.sync.dma_start(idx2[:], offs2)
+        nc.sync.dma_start(out=mem_cols[:], in_=mem.rearrange("o (p t) -> p (o t)", t=PLACES))
         nc.sync.dma_start(out=note_pool[1][:], in_=notes_by_place[:, 2:4, :])
-        nc.sync.dma_start(out=mem_cols[:], in_=mem.rearrange("o (p t) -> p (o t)", t=PACK))
         nc.sync.dma_start(out=given_pool[0][:], in_=given_by_place[:, 0, :])
         nc.sync.dma_start(idx3[:], offs3)
         nc.sync.dma_start(out=given_pool[1][:], in_=given_by_place[:, 1, :])
-        nc.sync.dma_start(out=rowf_cols[:], in_=rowf.rearrange("(p t) o -> p (t o)", t=PACK))
+        nc.sync.dma_start(out=rowf_cols[:], in_=rowf.rearrange("(p t) o -> p (t o)", t=PLACES))
         nc.sync.dma_start(out=given_pool[2][:], in_=given_by_place[:, 2, :])
         nc.sync.dma_start(out=given_pool[3][:], in_=given_by_place[:, 3, :])
-        for t in range(PACK):
+        for t in range(PLACES):
             nc.sync.dma_start(out=val_pool[t][:], in_=vals_by_place[:, t, :])
 
         shifted = sb.tile([P, N], F32, name="shifted")
@@ -109,40 +112,41 @@ def tile_attend_tab_timestable_changes_pl_kernel(
 
         key_listed = sb.tile([P, N], U16, name="key_listed")
         nc.vector.tensor_copy(key_listed[:], key_pool[:].indirect(idx[:]))
-        key_scales = sb.tile([P, PACK, P], U8, name="key_scales", align_bytes=64)
+        key_scales = sb.tile([P, PLACES, P], U8, name="key_scales", align_bytes=64)
         nc.vector.tensor_copy(key_scales[:].rearrange("p r s -> p s r"), key_scale_pool[:].indirect(idx[:]))
         key_words = sb.tile([P, 2 * N], U8, name="key_words", align_bytes=64)
         nc.vector.tensor_copy(
-            out=key_words[:].bitcast(U16).rearrange("p (r s) -> p r s", r=PACK),
-            in_=key_listed[:].rearrange("p (s r) -> p r s", r=PACK),
+            out=key_words[:].bitcast(U16).rearrange("p (r s) -> p r s", r=PLACES),
+            in_=key_listed[:].rearrange("p (s r) -> p r s", r=PLACES),
         )
 
-        note_planes = sb.tile([P, PACK, N], F32, name="note_planes")
-        note_grouped = sb.tile([P, N, PACK], BF16, name="note_grouped", align_bytes=64)
+        note_planes = sb.tile([P, PLACES, N], F32, name="note_planes")
+        note_grouped = sb.tile([P, N, PLACES], BF16, name="note_grouped", align_bytes=64)
         for u in range(2):
             nc.scalar.activation(note_planes[:, 2 * u, :], note_pool[u][:, 0, :].indirect(idx2[:]), COPY)
             nc.vector.tensor_copy(note_planes[:, 2 * u + 1, :], note_pool[u][:, 1, :].indirect(idx2[:]))
-            interleave_pair(nc.vector.tensor_copy, note_grouped, note_planes, slice(2 * u, 2 * u + 2))
+            for cols in HALVES:
+                group_pair(nc.vector.tensor_copy, note_grouped, note_planes, slice(2 * u, 2 * u + 2), cols)
         note_codes = sb.tile([P, N], U32, name="note_codes", align_bytes=64)
         note_scales = sb.tile([P, N], U8, name="note_scales", align_bytes=64)
         for cols in HALVES:
             quantise(nc, note_codes, note_scales, note_grouped, cols)
 
-        mem_turned = turn.tile([P, PACK, P], F32, name="mem_turned", tag="turn")
-        for c in range(PACK):
-            nc.tensor.transpose(mem_turned[:, c, :], mem_cols[:, c : c + 1].to_broadcast([P, P]), identity[:])
+        mem_turned = turn.tile([P, PLACES, P], F32, name="mem_turned", tag="turn")
+        for t in range(PLACES):
+            nc.tensor.transpose(mem_turned[:, t, :], mem_cols[:, t : t + 1].to_broadcast([P, P]), identity[:])
         mem_row = sb.tile([P, N], F32, name="mem_row")
-        nc.vector.tensor_copy(
-            out=mem_row[:].rearrange("p (n c) -> p n c", c=PACK), in_=mem_turned[:].rearrange("p c n -> p n c")
+        nc.scalar.copy(
+            out=mem_row[:].rearrange("p (n t) -> p n t", t=PLACES), in_=mem_turned[:].rearrange("p t n -> p n t")
         )
 
-        given_listed = sb.tile([P, PACK, N], F32, name="given_listed")
-        for r in range(PACK):
+        given_listed = sb.tile([P, PLACES, N], F32, name="given_listed")
+        for r in range(PLACES):
             nc.scalar.activation(given_listed[:, r, :], given_pool[r][:].indirect(idx3[:]), COPY)
 
-        table_grouped = sb.tile([P, N, PACK], BF16, name="table_grouped", align_bytes=64)
-        table_planes = sb.tile([P, PACK, N], BF16, name="table_planes")
-        for r in range(PACK):
+        table_grouped = sb.tile([P, N, PLACES], BF16, name="table_grouped", align_bytes=64)
+        table_planes = sb.tile([P, PLACES, N], BF16, name="table_planes")
+        for r in range(PLACES):
             g1 = acc.tile([P, N], F32, name="g1", tag="acc")
             nc.tensor.matmul_mx(
                 out=g1[:],
@@ -161,47 +165,46 @@ def tile_attend_tab_timestable_changes_pl_kernel(
                 op0=MULT,
                 op1=MULT,
             )
-        interleave(nc, table_grouped, table_planes)
+        group_planes(nc, table_grouped, table_planes)
         table_codes = sb.tile([P, N], U32, name="table_codes", align_bytes=64)
         table_scales = sb.tile([P, N], U8, name="table_scales", align_bytes=64)
         for cols in HALVES:
             quantise(nc, table_codes, table_scales, table_grouped, cols)
 
-        result = sb.tile([P, PACK, N], F32, name="result")
+        result = sb.tile([P, PLACES, N], F32, name="result")
         result_codes = sb.tile([P, N], U32, name="result_codes", align_bytes=64)
         result_scales = sb.tile([P, N], U8, name="result_scales", align_bytes=64)
-        last = PACK - 1
-        val_codes, val_scales = {}, {}
 
-        def prepare_values(t):
+        def turn_values(t):
             listed = sb.tile([P, N], BF16, name="val_listed%d" % t, tag="val_listed%d" % t, align_bytes=64)
             nc.scalar.activation(listed[:], val_pool[t][:].indirect(idx[:]), COPY)
-            pairs = listed[:].bitcast(F32)
-            turned = turn.tile([P, PACK, P], F32, name="val_turned", tag="turn")
+            words = listed[:].bitcast(F32)
+            turned = turn.tile([P, PLACES, P], F32, name="val_turned", tag="turn")
             for u in range(2):
-                nc.tensor.transpose(turned[:, u, :], pairs[:, u : N // 2 : 2], identity[:])
-            grouped = sb.tile([P, P * PACK], BF16, name="val_grouped%d" % t, align_bytes=64)
+                nc.tensor.transpose(turned[:, u, :], words[:, u : N // 2 : 2], identity[:])
+            val_grouped = sb.tile([P, P * PLACES], BF16, name="val_grouped%d" % t, align_bytes=64)
             copy_words = nc.scalar.copy if t % 2 else nc.vector.tensor_copy
             copy_words(
-                out=grouped[:].bitcast(F32).rearrange("s (p u) -> s p u", u=2),
+                out=val_grouped[:].bitcast(F32).rearrange("s (p u) -> s p u", u=2),
                 in_=turned[:, 0:2, :].rearrange("s u p -> s p u"),
             )
-            return grouped
+            return val_grouped
 
-        def quantise_values(t, grouped):
-            tag = "val_pool%d" % last if t == last - 1 else "val_codes%d" % t
-            val_codes[t] = sb.tile([P, P], U32, name="val_codes%d" % t, tag=tag, align_bytes=64)
-            val_scales[t] = sb.tile([P, P], U8, name="val_scales%d" % t, align_bytes=64)
-            nc.vector.quantize_mx(out=val_codes[t][:].bitcast(FP8X4), scales=val_scales[t][:], in_=grouped[:])
+        def quantise_values(t, val_grouped):
+            tag = "val_pool%d" % LAST if t == LAST - 1 else "val_codes%d" % t
+            codes = sb.tile([P, P], U32, name="val_codes%d" % t, tag=tag, align_bytes=64)
+            scales = sb.tile([P, P], U8, name="val_scales%d" % t, align_bytes=64)
+            nc.vector.quantize_mx(out=codes[:].bitcast(FP8X4), scales=scales[:], in_=val_grouped[:])
+            return codes, scales
 
-        def finish_rows(t):
+        def finish_plane(t, codes, scales):
             sums = []
             for cols in HALVES:
                 o = acc.tile([P, N], F32, name="o", tag="acc")
                 nc.tensor.matmul_mx(
                     out=o[:, 0:HALF],
-                    lhsT=val_codes[t][:].bitcast(FP8X4),
-                    lhsT_scale=val_scales[t][:],
+                    lhsT=codes[:].bitcast(FP8X4),
+                    lhsT_scale=scales[:],
                     rhs=table_codes[:, cols].bitcast(FP8X4),
                     rhs_scale=table_scales[:, cols],
                     start=True,
@@ -217,23 +220,25 @@ def tile_attend_tab_timestable_changes_pl_kernel(
                 nc.vector.tensor_tensor(result[:, t, cols], o[:, 0:HALF], shifted[:, cols], SUBTRACT)
             nc.sync.dma_start(out=out_by_place[:, t, :], in_=result[:, t, :])
 
-        grouped = [prepare_values(t) for t in range(PACK)]
-        for t in range(PACK):
-            quantise_values(t, grouped[t])
-        for t in range(PACK):
-            finish_rows(t)
+        turned_values = [turn_values(t) for t in range(PLACES)]
+        quantised_values = [quantise_values(t, turned_values[t]) for t in range(PLACES)]
+        for t in range(PLACES):
+            finish_plane(t, *quantised_values[t])
 
         result_grouped = sb.tile(
-            [P, N, PACK], BF16, name="result_grouped", tag="val_listed%d" % (PACK - 1), align_bytes=64
+            [P, N, PLACES], BF16, name="result_grouped", tag="val_listed%d" % LAST, align_bytes=64
         )
-        interleave_pair(nc.scalar.copy, result_grouped, result, slice(0, 2))
-        interleave_pair(nc.vector.tensor_copy, result_grouped, result, slice(2, 4))
+        for cols in HALVES:
+            group_pair(nc.scalar.copy, result_grouped, result, slice(0, 2), cols)
+        group_pair(nc.scalar.copy, result_grouped, result, slice(2, 4), slice(0, SCALAR_SHARE))
+        group_pair(nc.vector.tensor_copy, result_grouped, result, slice(2, 4), slice(SCALAR_SHARE, HALF))
+        group_pair(nc.vector.tensor_copy, result_grouped, result, slice(2, 4), slice(HALF, N))
 
         words_out = out_1[0].rearrange("p c r -> p (c r)").bitcast(I32)
         for cols in HALVES:
             quantise(nc, result_codes, result_scales, result_grouped, cols)
             nc.sync.dma_start(out=words_out[:, cols], in_=result_codes[:, cols].bitcast(I32))
-        for q in range(4):
+        for q in range(QUADRANTS):
             queue = nc.scalar if q else nc.sync
             queue.dma_start(
                 out=out_2[0, 4 * q : 4 * q + 4, :].bitcast(I32),

from contextlib import ExitStack

import concourse.mybir as mybir
from concourse.masks import make_identity

FLOPS = 2 * 2 * 512 * 512 * 512

F32 = mybir.dt.float32
BF16 = mybir.dt.bfloat16
I32 = mybir.dt.int32
U32 = mybir.dt.uint32
U16 = mybir.dt.uint16
U8 = mybir.dt.uint8
FP8X4 = mybir.dt.float8_e4m3fn_x4
FP4X4 = mybir.dt.float4_e2m1fn_x4
MULT = mybir.AluOpType.mult
SUBTRACT = mybir.AluOpType.subtract
COPY = mybir.ActivationFunctionType.Copy

P = 128
PLACES = 4
LAST = PLACES - 1
QUADRANTS = 4
N = 512
TOKENS = 2048
NOTES = 1024
WIDE = 1024

HALF = N // 2
HALVES = [slice(0, HALF), slice(HALF, N)]
SCALAR_SHARE = N // 4
SUM_BANKS = 6
TURN_BANKS = 2


def group_planes(nc, grouped, planes):
    for cols in HALVES:
        nc.vector.tensor_copy(
            out=grouped[:, cols, :].rearrange("p (c i) t -> p c t i", i=4),
            in_=planes[:, :, cols].rearrange("p t (c i) -> p c t i", i=4),
        )


def group_pair(copy, grouped, planes, pair, cols):
    copy(out=grouped[:, cols, pair], in_=planes[:, pair, cols].rearrange("p t j -> p j t"))


def quantise(nc, codes, scales, grouped, cols):
    nc.vector.quantize_mx(
        out=codes[:, cols].bitcast(FP8X4),
        scales=scales[:, cols],
        in_=grouped[:, cols, :].rearrange("p j t -> p (j t)"),
    )


def tile_attend_tab_timestable_changes_pl_kernel(
    tc, keys_words, keys_scales, notes, given, rowf, vals, mem, offs, offs2, offs3, out_0, out_1, out_2
):
    nc = tc.nc
    with ExitStack() as ctx:
        sb = ctx.enter_context(tc.tile_pool(name="sb", bufs=1))
        acc = ctx.enter_context(tc.psum_pool(name="acc", bufs=SUM_BANKS))
        turn = ctx.enter_context(tc.psum_pool(name="turn", bufs=TURN_BANKS))

        idx = sb.tile([P, N // 16], U16, name="idx")
        idx2 = sb.tile([P, N // 16], U16, name="idx2")
        idx3 = sb.tile([P, N // 16], U16, name="idx3")
        key_pool = sb.tile([P, TOKENS], U16, name="key_pool")
        key_scale_pool = sb.tile([P, TOKENS], U8, name="key_scale_pool")
        note_pool = [sb.tile([P, 2, NOTES], F32, name="note_pool%d" % u) for u in range(2)]
        given_pool = [sb.tile([P, WIDE], F32, name="given_pool%d" % t) for t in range(PLACES)]
        val_pool = [
            sb.tile([P, TOKENS], F32, name="val_pool%d" % t, tag="val_pool%d" % t, align_bytes=64)
            for t in range(PLACES)
        ]
        rowf_cols = sb.tile([P, PLACES], F32, name="rowf_cols")
        mem_cols = sb.tile([P, PLACES], F32, name="mem_cols")

        notes_by_place = notes.rearrange("(p t) u -> p t u", t=PLACES)
        given_by_place = given.rearrange("(p t) z -> p t z", t=PLACES)
        vals_by_place = vals.rearrange("(p t) c -> p t c", t=PLACES)
        out_by_place = out_0.rearrange("(p t) j -> p t j", t=PLACES)

        zero = sb.tile([P, 1], F32, name="zero")
        nc.vector.memset(zero[:], 0.0)
        nc.vector.memset(key_scale_pool[:].bitcast(I32), 0)
        identity = sb.tile([P, P], F32, name="identity")
        make_identity(nc, identity[:])

        nc.sync.dma_start(idx[:], offs)
        nc.sync.dma_start(out=key_pool[:].bitcast(I32), in_=keys_words[0].bitcast(I32))
        for q in range(QUADRANTS):
            nc.sync.dma_start(
                out=key_scale_pool[32 * q : 32 * q + 4, :].bitcast(I32),
                in_=keys_scales[0, 4 * q : 4 * q + 4, :].bitcast(I32),
            )
        nc.sync.dma_start(out=note_pool[0][:], in_=notes_by_place[:, 0:2, :])
        nc.sync.dma_start(idx2[:], offs2)
        nc.sync.dma_start(out=mem_cols[:], in_=mem.rearrange("o (p t) -> p (o t)", t=PLACES))
        nc.sync.dma_start(out=note_pool[1][:], in_=notes_by_place[:, 2:4, :])
        nc.sync.dma_start(out=given_pool[0][:], in_=given_by_place[:, 0, :])
        nc.sync.dma_start(idx3[:], offs3)
        nc.sync.dma_start(out=given_pool[1][:], in_=given_by_place[:, 1, :])
        nc.sync.dma_start(out=rowf_cols[:], in_=rowf.rearrange("(p t) o -> p (t o)", t=PLACES))
        nc.sync.dma_start(out=given_pool[2][:], in_=given_by_place[:, 2, :])
        nc.sync.dma_start(out=given_pool[3][:], in_=given_by_place[:, 3, :])
        for t in range(PLACES):
            nc.sync.dma_start(out=val_pool[t][:], in_=vals_by_place[:, t, :])

        shifted = sb.tile([P, N], F32, name="shifted")
        nc.scalar.activation(shifted[:, 0:1], zero[:], COPY)

        key_listed = sb.tile([P, N], U16, name="key_listed")
        nc.vector.tensor_copy(key_listed[:], key_pool[:].indirect(idx[:]))
        key_scales = sb.tile([P, PLACES, P], U8, name="key_scales", align_bytes=64)
        nc.vector.tensor_copy(key_scales[:].rearrange("p r s -> p s r"), key_scale_pool[:].indirect(idx[:]))
        key_words = sb.tile([P, 2 * N], U8, name="key_words", align_bytes=64)
        nc.vector.tensor_copy(
            out=key_words[:].bitcast(U16).rearrange("p (r s) -> p r s", r=PLACES),
            in_=key_listed[:].rearrange("p (s r) -> p r s", r=PLACES),
        )

        note_planes = sb.tile([P, PLACES, N], F32, name="note_planes")
        note_grouped = sb.tile([P, N, PLACES], BF16, name="note_grouped", align_bytes=64)
        for u in range(2):
            nc.scalar.activation(note_planes[:, 2 * u, :], note_pool[u][:, 0, :].indirect(idx2[:]), COPY)
            nc.vector.tensor_copy(note_planes[:, 2 * u + 1, :], note_pool[u][:, 1, :].indirect(idx2[:]))
            for cols in HALVES:
                group_pair(nc.vector.tensor_copy, note_grouped, note_planes, slice(2 * u, 2 * u + 2), cols)
        note_codes = sb.tile([P, N], U32, name="note_codes", align_bytes=64)
        note_scales = sb.tile([P, N], U8, name="note_scales", align_bytes=64)
        for cols in HALVES:
            quantise(nc, note_codes, note_scales, note_grouped, cols)

        mem_turned = turn.tile([P, PLACES, P], F32, name="mem_turned", tag="turn")
        for t in range(PLACES):
            nc.tensor.transpose(mem_turned[:, t, :], mem_cols[:, t : t + 1].to_broadcast([P, P]), identity[:])
        mem_row = sb.tile([P, N], F32, name="mem_row")
        nc.scalar.copy(
            out=mem_row[:].rearrange("p (n t) -> p n t", t=PLACES), in_=mem_turned[:].rearrange("p t n -> p n t")
        )

        given_listed = sb.tile([P, PLACES, N], F32, name="given_listed")
        for r in range(PLACES):
            nc.scalar.activation(given_listed[:, r, :], given_pool[r][:].indirect(idx3[:]), COPY)

        table_grouped = sb.tile([P, N, PLACES], BF16, name="table_grouped", align_bytes=64)
        table_planes = sb.tile([P, PLACES, N], BF16, name="table_planes")
        for r in range(PLACES):
            g1 = acc.tile([P, N], F32, name="g1", tag="acc")
            nc.tensor.matmul_mx(
                out=g1[:],
                lhsT=key_words[:, 2 * P * r : 2 * P * (r + 1)].bitcast(FP4X4),
                lhsT_scale=key_scales[:, r, :],
                rhs=note_codes[:].bitcast(FP8X4),
                rhs_scale=note_scales[:],
                start=True,
                stop=True,
            )
            nc.vector.scalar_tensor_tensor(
                out=table_planes[:, r, :],
                in0=g1[:],
                scalar=rowf_cols[:, r : r + 1],
                in1=given_listed[:, r, :],
                op0=MULT,
                op1=MULT,
            )
        group_planes(nc, table_grouped, table_planes)
        table_codes = sb.tile([P, N], U32, name="table_codes", align_bytes=64)
        table_scales = sb.tile([P, N], U8, name="table_scales", align_bytes=64)
        for cols in HALVES:
            quantise(nc, table_codes, table_scales, table_grouped, cols)

        result = sb.tile([P, PLACES, N], F32, name="result")
        result_codes = sb.tile([P, N], U32, name="result_codes", align_bytes=64)
        result_scales = sb.tile([P, N], U8, name="result_scales", align_bytes=64)

        def turn_values(t):
            listed = sb.tile([P, N], BF16, name="val_listed%d" % t, tag="val_listed%d" % t, align_bytes=64)
            nc.scalar.activation(listed[:], val_pool[t][:].indirect(idx[:]), COPY)
            words = listed[:].bitcast(F32)
            turned = turn.tile([P, PLACES, P], F32, name="val_turned", tag="turn")
            for u in range(2):
                nc.tensor.transpose(turned[:, u, :], words[:, u : N // 2 : 2], identity[:])
            val_grouped = sb.tile([P, P * PLACES], BF16, name="val_grouped%d" % t, align_bytes=64)
            copy_words = nc.scalar.copy if t % 2 else nc.vector.tensor_copy
            copy_words(
                out=val_grouped[:].bitcast(F32).rearrange("s (p u) -> s p u", u=2),
                in_=turned[:, 0:2, :].rearrange("s u p -> s p u"),
            )
            return val_grouped

        def quantise_values(t, val_grouped):
            tag = "val_pool%d" % LAST if t == LAST - 1 else "val_codes%d" % t
            codes = sb.tile([P, P], U32, name="val_codes%d" % t, tag=tag, align_bytes=64)
            scales = sb.tile([P, P], U8, name="val_scales%d" % t, align_bytes=64)
            nc.vector.quantize_mx(out=codes[:].bitcast(FP8X4), scales=scales[:], in_=val_grouped[:])
            return codes, scales

        def finish_plane(t, codes, scales):
            sums = []
            for cols in HALVES:
                o = acc.tile([P, N], F32, name="o", tag="acc")
                nc.tensor.matmul_mx(
                    out=o[:, 0:HALF],
                    lhsT=codes[:].bitcast(FP8X4),
                    lhsT_scale=scales[:],
                    rhs=table_codes[:, cols].bitcast(FP8X4),
                    rhs_scale=table_scales[:, cols],
                    start=True,
                    stop=True,
                )
                sums.append(o)
            for cols, o in zip(HALVES, sums):
                after = slice(cols.start + 1, min(cols.stop + 1, N))
                nc.vector.tensor_tensor(
                    shifted[:, after], o[:, 0 : after.stop - after.start], mem_row[:, after], MULT
                )
            for cols, o in zip(HALVES, sums):
                nc.vector.tensor_tensor(result[:, t, cols], o[:, 0:HALF], shifted[:, cols], SUBTRACT)
            nc.sync.dma_start(out=out_by_place[:, t, :], in_=result[:, t, :])

        turned_values = [turn_values(t) for t in range(PLACES)]
        quantised_values = [quantise_values(t, turned_values[t]) for t in range(PLACES)]
        for t in range(PLACES):
            finish_plane(t, *quantised_values[t])

        result_grouped = sb.tile(
            [P, N, PLACES], BF16, name="result_grouped", tag="val_listed%d" % LAST, align_bytes=64
        )
        for cols in HALVES:
            group_pair(nc.scalar.copy, result_grouped, result, slice(0, 2), cols)
        group_pair(nc.scalar.copy, result_grouped, result, slice(2, 4), slice(0, SCALAR_SHARE))
        group_pair(nc.vector.tensor_copy, result_grouped, result, slice(2, 4), slice(SCALAR_SHARE, HALF))
        group_pair(nc.vector.tensor_copy, result_grouped, result, slice(2, 4), slice(HALF, N))

        words_out = out_1[0].rearrange("p c r -> p (c r)").bitcast(I32)
        for cols in HALVES:
            quantise(nc, result_codes, result_scales, result_grouped, cols)
            nc.sync.dma_start(out=words_out[:, cols], in_=result_codes[:, cols].bitcast(I32))
        for q in range(QUADRANTS):
            queue = nc.scalar if q else nc.sync
            queue.dma_start(
                out=out_2[0, 4 * q : 4 * q + 4, :].bitcast(I32),
                in_=result_scales[32 * q : 32 * q + 4, :].bitcast(I32),
            )
